import numpy as np
import ml_dtypes


def mxq(x, axis, fmt="e4m3"):
    dtype, down = {"e4m3": (ml_dtypes.float8_e4m3fn, 7), "e5m2": (ml_dtypes.float8_e5m2, 14)}[fmt]
    v = np.moveaxis(np.asarray(x, np.float32).astype(ml_dtypes.bfloat16).astype(np.float64), axis, -1)
    blocks = v.reshape(v.shape[:-1] + (-1, 32))
    amax = np.abs(blocks).max(-1, keepdims=True)
    byte = np.maximum(np.where(amax > 0, np.frexp(amax)[1] - 1 + 127, 0) - down, 1)
    scale = np.exp2(byte - 127.0)
    codes = (blocks / scale).astype(np.float32).astype(dtype).astype(np.float64)
    return np.moveaxis((codes * scale).reshape(v.shape), -1, axis)


WIDE = False


def mx_kscale(k):
    if not WIDE:
        return np.ones(k)
    levels = np.array([10, -10, 5, -5, 0])
    if k % 512:
        return np.exp2(np.random.permutation(np.resize(levels, k // 32))).repeat(32)
    a = np.empty((k // 512, 16))
    for p in range(k // 512):
        a[p, :8] = np.random.permutation(np.resize(levels, 8))
        for g in range(8):
            far = levels[np.abs(levels - a[p, g]) >= 10]
            a[p, g + 8] = far[np.random.randint(len(far))]
    return np.exp2(a.ravel()).repeat(32)


def f64(x):
    return np.asarray(x).astype(np.float64)


def striped(idx):
    return np.tile(idx.reshape(-1, 16).T, (8, 1)).astype(np.uint16)


def unstriped(offs):
    return offs[:16].T.reshape(-1).astype(np.int64)


def striped8(idx):
    return np.concatenate([x.reshape(-1, 16).T for x in idx]).astype(np.uint16)


def runs(offs, k):
    lists = np.stack([offs[16 * r : 16 * r + 16].T.reshape(-1) for r in range(8)]).astype(np.int64)
    return lists[np.arange(k) % 512 // 64]


def pack_weight(w):
    k, n = w.shape
    w = f64(np.asarray(w, np.float32).astype(ml_dtypes.bfloat16)).reshape(k // 32, 32, n)
    amax = np.abs(w).max(1)
    byte = np.clip(np.where(amax > 0, np.frexp(amax)[1] - 1 + 127 - 7, 1), 1, 254)
    scaled = (w * np.exp2(127.0 - byte)[:, None, :]).reshape(k, n).astype(np.float32)
    words = np.ascontiguousarray(scaled.reshape(k // 512, 128, 4, n).transpose(0, 1, 3, 2)).astype(ml_dtypes.float8_e4m3fn).view(np.uint8)
    return words, np.ascontiguousarray(byte.astype(np.uint8).reshape(k // 512, 16, n))


def unpack_weight(words, scales):
    g, p, n, _ = words.shape
    vals = np.ascontiguousarray(words).view(ml_dtypes.float8_e4m3fn).astype(np.float64) * np.repeat(np.exp2(scales.astype(np.float64) - 127.0), 8, axis=1)[..., None]
    return vals.transpose(0, 1, 3, 2).reshape(g * 512, n)


E2M1 = np.array([0.0, 0.5, 1.0, 1.5, 2.0, 3.0, 4.0, 6.0, -0.0, -0.5, -1.0, -1.5, -2.0, -3.0, -4.0, -6.0])


def pack_fp4(w):
    k, n = w.shape
    w = f64(np.asarray(w, np.float32).astype(ml_dtypes.bfloat16)).reshape(k // 32, 32, n)
    amax = np.abs(w).max(1)
    mant, ex = np.frexp(amax / 6.0)
    byte = np.clip(np.where(amax > 0, np.where(mant > 0.5, ex, ex - 1) + 127, 1), 1, 254)
    scaled = (w * np.exp2(127.0 - byte)[:, None, :]).reshape(k, n).astype(np.float32)
    c = np.ascontiguousarray(scaled.reshape(k // 512, 128, 4, n).transpose(0, 1, 3, 2)).astype(ml_dtypes.float4_e2m1fn).view(np.uint8) & 0xF
    words = (c[..., 0::2] | (c[..., 1::2] << 4)).reshape(k // 512, 128, 2 * n)
    return np.ascontiguousarray(words), np.ascontiguousarray(byte.astype(np.uint8).reshape(k // 512, 16, n))


def unpack_fp4(words, scales):
    g, _, n = scales.shape
    words = np.ascontiguousarray(words).reshape(g, 128, n, 2)
    nib = np.empty((g, 128, n, 4), np.uint8)
    nib[..., 0::2] = words & 0xF
    nib[..., 1::2] = words >> 4
    vals = E2M1[nib] * np.repeat(np.exp2(scales.astype(np.float64) - 127.0), 8, axis=1)[..., None]
    return vals.transpose(0, 1, 3, 2).reshape(g * 512, n)


def relu(v):
    return np.maximum(v, 0.0)

def planes(y):
    n, m = y.shape
    v = y.astype(np.float32).astype(ml_dtypes.bfloat16).astype(np.float64).reshape(n // 32, 32, m)
    top = np.abs(v).max(1)
    byte = np.clip(np.where(top > 0, np.frexp(top)[1] - 1 + 127 - 7, 1), 1, 254)
    codes = (v * np.exp2(127.0 - byte)[:, None, :]).reshape(n, m).astype(np.float32).astype(ml_dtypes.float8_e4m3fn).view(np.uint8)
    words = codes.reshape(n // 512, 128, 4, m).transpose(0, 1, 3, 2)
    return np.ascontiguousarray(words), np.ascontiguousarray(byte.astype(np.uint8).reshape(n // 512, 16, m))


K, T, S, H, G = 512, 2048, 512, 512, 2048


def setup_inputs():
    n = np.random.standard_normal
    s = mx_kscale(K)[:, None]
    packed_xT = pack_weight(n((K, T)) * s)
    packed_w1 = pack_fp4(n((K, H)) / np.sqrt(K) / s)
    packed_dT = pack_weight(n((K, G)) / s)
    return {
        "x_words": packed_xT[0],
        "x_scales": packed_xT[1],
        "w1_words": packed_w1[0],
        "w1_scales": packed_w1[1],
        "gs": (np.random.uniform(0.5, 1.5, (K, 1)) * s).astype(np.float32),
        "d_words": packed_dT[0],
        "d_scales": packed_dT[1],
        "offs": striped(np.random.permutation(T)[:S]),
        "n1": striped8(np.stack([np.random.permutation(S) for _ in range(8)])),
        "n2": striped8(np.stack([np.random.permutation(S) for _ in range(8)])),
        "k1": striped8(np.random.randint(0, G, (8, H))),
        "n3": striped8(np.stack([np.random.permutation(S) for _ in range(8)])),
        "n4": striped8(np.stack([np.random.permutation(S) for _ in range(8)])),
    }


def reference(x_words, x_scales, w1_words, w1_scales, gs, d_words, d_scales, offs, n1, n2, k1, n3, n4):
    d_k1 = unpack_weight(d_words, d_scales)[np.arange(K)[:, None], runs(k1, K)]
    xq = unpack_weight(x_words, x_scales)[:, unstriped(offs)]
    y = unpack_fp4(w1_words, w1_scales).T @ xq
    pa = y - (y[np.arange(H)[:, None], runs(n1, H)])
    pb = y[np.arange(H)[:, None], runs(n2, H)] - y
    z = f64(gs) * (relu(np.minimum(pa, pb)) - (relu(-1.0 * np.maximum(pa, pb))))
    h = 0.0625 * ((d_k1.T @ mxq(z, 0, "e4m3")))
    out_0 = np.maximum(h[np.arange(H)[:, None], runs(n3, H)], h[np.arange(H)[:, None], runs(n4, H)]) - (0.75 * h)
    return (out_0,) + planes(out_0)

@@ -1,0 +1,249 @@
+from contextlib import ExitStack
+
+import concourse.mybir as mybir
+
+F32 = mybir.dt.float32
+BF16 = mybir.dt.bfloat16
+I32 = mybir.dt.int32
+U32 = mybir.dt.uint32
+U16 = mybir.dt.uint16
+U8 = mybir.dt.uint8
+FP8X4 = mybir.dt.float8_e4m3fn_x4
+FP4X4 = mybir.dt.float4_e2m1fn_x4
+ALU = mybir.AluOpType
+COPY = mybir.ActivationFunctionType.Copy
+
+P = 128
+PACK = 4
+S = 512
+TABLE = 2048
+FLOPS = 2 * 2 * 512 * 512 * 512
+
+FIRST_CHUNKS = ((0, 256), (256, 256))
+SECOND_CHUNKS = ((0, 256), (256, 128), (384, 128))
+VECTOR_FETCHES = 4
+
+
+def entries(lst, start, width):
+    return lst[:, start // 16 : (start + width) // 16]
+
+
+def interleave(nc, dst, src):
+    nc.vector.tensor_copy(
+        out=dst[:].rearrange("p (c i) t -> p c t i", i=4),
+        in_=src[:].rearrange("p t (c i) -> p c t i", i=4),
+    )
+
+
+def tile_picked_denseminmodover_none_po_kernel(
+    tc, x_words, x_scales, w1_words, w1_scales, gs, d_words, d_scales, offs, n1, n2, k1, n3, n4, out_0, out_1, out_2
+):
+    nc = tc.nc
+    with ExitStack() as ctx:
+        keep = ctx.enter_context(tc.tile_pool(name="keep", bufs=1))
+        psum = ctx.enter_context(tc.psum_pool(name="psum", bufs=1))
+
+        def held(name, shape, dtype):
+            return keep.tile(shape, dtype, name=name, align_bytes=64)
+
+        def bank(number, name, width):
+            return psum.tile([P, width], F32, name=name, tag="bank%d" % (number % 8))
+
+        lists = {}
+        for name in ("offs", "n1", "n2", "k1", "n3", "n4"):
+            lists[name] = held("list_" + name, [P, S // 16], U16)
+
+        x_table = held("x_table", [P, TABLE], I32)
+        x_byte_table = held("x_byte_table", [P, TABLE], U8)
+        d_table = held("d_table", [P, TABLE], I32)
+        d_byte_table = held("d_byte_table", [P, TABLE], U8)
+        w_raw = held("w_raw", [P, 2 * S], U8)
+        w_byte_raw = held("w_byte_raw", [P, S], U8)
+        gain = held("gain", [P, PACK], F32)
+        d_bytes = held("d_bytes", [P, S], U8)
+
+        nc.gpsimd.memset(x_byte_table[:].bitcast(I32), 0)
+        nc.gpsimd.memset(w_byte_raw[:].bitcast(I32), 0)
+        nc.vector.memset(d_byte_table[:].bitcast(I32), 0)
+        nc.vector.memset(d_bytes[:].bitcast(I32), 0)
+
+        nc.sync.dma_start(lists["offs"][:], offs)
+        for q in range(4):
+            nc.scalar.dma_start(
+                x_byte_table[32 * q : 32 * q + 4, :].bitcast(I32), x_scales[0, 4 * q : 4 * q + 4, :].bitcast(I32)
+            )
+        nc.sync.dma_start(w_raw[:].bitcast(I32), w1_words[0].bitcast(I32))
+        nc.sync.dma_start(x_table[:], x_words[0].rearrange("p n t -> p (n t)").bitcast(I32))
+        for q in range(4):
+            nc.scalar.dma_start(
+                w_byte_raw[32 * q : 32 * q + 4, :].bitcast(I32), w1_scales[0, 4 * q : 4 * q + 4, :].bitcast(I32)
+            )
+        nc.sync.dma_start(gain[:], gs.rearrange("(p t) o -> p (t o)", t=PACK))
+        nc.sync.dma_start(lists["n1"][:], n1)
+        nc.sync.dma_start(lists["n2"][:], n2)
+        nc.sync.dma_start(d_table[:], d_words[0].rearrange("p n t -> p (n t)").bitcast(I32))
+        nc.sync.dma_start(lists["k1"][:], k1)
+        nc.sync.dma_start(d_byte_table[0:P:8, :].bitcast(I32), d_scales[0].bitcast(I32))
+        nc.sync.dma_start(lists["n3"][:], n3)
+        nc.sync.dma_start(lists["n4"][:], n4)
+
+        x_bytes = held("x_bytes", [P, S], U8)
+        nc.vector.tensor_copy(x_bytes[:], x_byte_table[:].indirect(lists["offs"][:]))
+        w_codes = held("w_codes", [P, 2 * S], U8)
+        nc.scalar.copy(
+            w_codes[:].bitcast(U16).rearrange("p (t m) -> p t m", t=PACK),
+            w_raw[:].bitcast(U16).rearrange("p (m t) -> p t m", t=PACK),
+        )
+        w_bytes = held("w_bytes", [P, S], U8)
+        nc.vector.tensor_copy(
+            w_bytes[:].rearrange("p (t m) -> p t m", t=PACK), w_byte_raw[:].rearrange("p (m t) -> p t m", t=PACK)
+        )
+        x_codes = held("x_codes", [P, S], U32)
+        nc.vector.tensor_copy(x_codes[:], x_table[:].bitcast(U32).indirect(lists["offs"][:]))
+
+        y = []
+        for t in range(PACK):
+            acc = bank(t, "y_acc%d" % t, S)
+            nc.tensor.matmul_mx(
+                acc[:],
+                lhsT=w_codes[:, 2 * P * t : 2 * P * (t + 1)].bitcast(FP4X4),
+                lhsT_scale=w_bytes[:, P * t : P * (t + 1)],
+                rhs=x_codes[:].bitcast(FP8X4),
+                rhs_scale=x_bytes[:],
+                start=True,
+                stop=True,
+            )
+            row = held("y%d" % t, [P, S], F32)
+            if t == 1:
+                nc.vector.tensor_scalar(row[:], acc[:], gain[:, t : t + 1], None, ALU.mult)
+            else:
+                nc.scalar.activation(row[:], acc[:], COPY, scale=gain[:, t : t + 1])
+            y.append(row)
+
+        d_picked_bytes = held("d_picked_bytes", [P, S], U8)
+        nc.vector.tensor_copy(d_picked_bytes[:], d_byte_table[:].indirect(lists["k1"][:]))
+        d_picked = held("d_picked", [P, S], U32)
+        nc.vector.tensor_copy(d_picked[:], d_table[:].bitcast(U32).indirect(lists["k1"][:]))
+        d_dealt_bytes = held("d_dealt_bytes", [P, S], U8)
+        nc.vector.tensor_copy(
+            d_dealt_bytes[:].rearrange("p (t m) -> p t m", t=PACK),
+            d_picked_bytes[:].rearrange("p (m t) -> p t m", t=PACK),
+        )
+        for r in range(4):
+            nc.sync.dma_start(d_bytes[r:P:32, :].bitcast(I32), d_dealt_bytes[8 * r : P : 32, :].bitcast(I32))
+        d_codes = held("d_codes", [P, S], U32)
+        nc.vector.tensor_copy(
+            d_codes[:].rearrange("p (t m) -> p m t", t=PACK), d_picked[:].rearrange("p (m t) -> p m t", t=PACK)
+        )
+
+        h = [held("h%d" % t, [P, S], F32) for t in range(PACK)]
+        z_codes = held("z_codes", [P, S], U32)
+        z_bytes = held("z_bytes", [P, S], U8)
+
+        steps = [(c, t) for c in range(len(FIRST_CHUNKS)) for t in range(PACK)]
+        pa, pb, low, z_rows = {}, {}, {}, {}
+
+        def fetch_first(c, t):
+            start, width = FIRST_CHUNKS[c]
+            a = held("a%d_%d" % (c, t), [P, width], F32)
+            b = held("b%d_%d" % (c, t), [P, width], F32)
+            nc.scalar.activation(a[:], y[t][:].indirect(entries(lists["n1"], start, width)), COPY)
+            nc.scalar.activation(b[:], y[t][:].indirect(entries(lists["n2"], start, width)), COPY)
+            return a, b
+
+        def clamp_low(c, t):
+            width = FIRST_CHUNKS[c][1]
+            low[c, t] = held("low%d_%d" % (c, t), [P, width], F32)
+            nc.vector.scalar_tensor_tensor(low[c, t][:], pa[c, t][:], 0.0, pb[c, t][:], ALU.min, ALU.max)
+
+        def clamp_high(c, t):
+            start, width = FIRST_CHUNKS[c]
+            if t == 0:
+                z_rows[c] = held("z_rows%d" % c, [P, PACK, width], BF16)
+            nc.vector.scalar_tensor_tensor(z_rows[c][:, t, :], pa[c, t][:], 0.0, low[c, t][:], ALU.max, ALU.min)
+            if t == PACK - 1:
+                second_product(c)
+
+        def second_product(c):
+            start, width = FIRST_CHUNKS[c]
+            cols = slice(start, start + width)
+            grouped = held("z_grouped%d" % c, [P, width, PACK], BF16)
+            interleave(nc, grouped, z_rows[c])
+            nc.vector.quantize_mx(
+                z_codes[:, cols].bitcast(FP8X4), z_bytes[:, cols], grouped[:].rearrange("p j t -> p (j t)")
+            )
+            for t in range(PACK):
+                acc = bank(4 + 4 * c + t, "h_acc%d_%d" % (c, t), width)
+                nc.tensor.matmul_mx(
+                    acc[:],
+                    lhsT=d_codes[:, P * t : P * (t + 1)].bitcast(FP8X4),
+                    lhsT_scale=d_bytes[:, P * t : P * (t + 1)],
+                    rhs=z_codes[:, cols].bitcast(FP8X4),
+                    rhs_scale=z_bytes[:, cols],
+                    start=True,
+                    stop=True,
+                )
+                if c == len(FIRST_CHUNKS) - 1 and t % 2 == 1:
+                    nc.vector.tensor_scalar(h[t][:, cols], acc[:], 0.0625, None, ALU.mult)
+                else:
+                    nc.scalar.activation(h[t][:, cols], acc[:], COPY, scale=0.0625)
+
+        for s in range(len(steps) + 2):
+            if s < len(steps):
+                c, t = steps[s]
+                start, width = FIRST_CHUNKS[c]
+                cols = slice(start, start + width)
+                a, b = fetch_first(c, t)
+                pa[c, t] = held("pa%d_%d" % (c, t), [P, width], F32)
+                pb[c, t] = held("pb%d_%d" % (c, t), [P, width], F32)
+                nc.vector.tensor_tensor(pa[c, t][:], y[t][:, cols], a[:], ALU.subtract)
+            if s >= 2:
+                clamp_high(*steps[s - 2])
+            if s < len(steps):
+                nc.vector.tensor_tensor(pb[c, t][:], b[:], y[t][:, cols], ALU.subtract)
+            if 1 <= s <= len(steps):
+                clamp_low(*steps[s - 1])
+
+        out_codes = held("out_codes", [P, S], U32)
+        out_bytes = held("out_bytes", [P, S], U8)
+        out_rows = out_0.rearrange("(p t) j -> p t j", t=PACK)
+        out_words = out_1[0].rearrange("p n t -> p (n t)").bitcast(I32)
+        steps = [(c, t) for c in range(len(SECOND_CHUNKS)) for t in range(PACK)]
+        larger, result = {}, {}
+
+        def finish(c, t):
+            start, width = SECOND_CHUNKS[c]
+            cols = slice(start, start + width)
+            if t == 0:
+                result[c] = held("result%d" % c, [P, PACK, width], F32)
+            nc.vector.scalar_tensor_tensor(result[c][:, t, :], h[t][:, cols], -0.75, larger[c, t][:], ALU.mult, ALU.add)
+            if t == PACK - 1:
+                nc.sync.dma_start(out_rows[:, :, cols], result[c][:])
+                grouped = held("out_grouped%d" % c, [P, width, PACK], BF16)
+                interleave(nc, grouped, result[c])
+                nc.vector.quantize_mx(
+                    out_codes[:, cols].bitcast(FP8X4), out_bytes[:, cols], grouped[:].rearrange("p j t -> p (j t)")
+                )
+                nc.sync.dma_start(out_words[:, cols], out_codes[:, cols].bitcast(I32))
+
+        for s in range(len(steps) + 1):
+            if s < len(steps):
+                c, t = steps[s]
+                start, width = SECOND_CHUNKS[c]
+                third = held("third%d_%d" % (c, t), [P, width], F32)
+                fourth = held("fourth%d_%d" % (c, t), [P, width], F32)
+                nc.scalar.activation(third[:], h[t][:].indirect(entries(lists["n3"], start, width)), COPY)
+                if s < VECTOR_FETCHES:
+                    nc.vector.tensor_copy(fourth[:], h[t][:].indirect(entries(lists["n4"], start, width)))
+                else:
+                    nc.scalar.activation(fourth[:], h[t][:].indirect(entries(lists["n4"], start, width)), COPY)
+                larger[c, t] = held("larger%d_%d" % (c, t), [P, width], F32)
+                nc.vector.tensor_tensor(larger[c, t][:], third[:], fourth[:], ALU.max)
+            if s >= 1:
+                finish(*steps[s - 1])
+
+        for q in range(4):
+            queue = nc.sync if q % 2 == 0 else nc.scalar
+            queue.dma_start(
+                out_2[0, 4 * q : 4 * q + 4, :].bitcast(I32), out_bytes[32 * q : 32 * q + 4, :].bitcast(I32)
+            )

@@ -19,20 +19,8 @@ S = 512
 TABLE = 2048
 FLOPS = 2 * 2 * 512 * 512 * 512
 
-FIRST_CHUNKS = ((0, 256), (256, 256))
-SECOND_CHUNKS = ((0, 256), (256, 128), (384, 128))
-VECTOR_FETCHES = 4
-
-
-def entries(lst, start, width):
-    return lst[:, start // 16 : (start + width) // 16]
-
-
-def interleave(nc, dst, src):
-    nc.vector.tensor_copy(
-        out=dst[:].rearrange("p (c i) t -> p c t i", i=4),
-        in_=src[:].rearrange("p t (c i) -> p c t i", i=4),
-    )
+LAST = PACK - 1
+HALF = S // 2
 
 
 def tile_picked_denseminmodover_none_po_kernel(
@@ -43,22 +31,22 @@ def tile_picked_denseminmodover_none_po_kernel(
         keep = ctx.enter_context(tc.tile_pool(name="keep", bufs=1))
         psum = ctx.enter_context(tc.psum_pool(name="psum", bufs=1))
 
-        def held(name, shape, dtype):
-            return keep.tile(shape, dtype, name=name, align_bytes=64)
+        def held(name, shape, dtype, tag=None):
+            return keep.tile(shape, dtype, name=name, tag=tag or name, align_bytes=64)
 
-        def bank(number, name, width):
-            return psum.tile([P, width], F32, name=name, tag="bank%d" % (number % 8))
+        def bank(number, name, shape):
+            return psum.tile(shape, F32, name=name, tag="bank%d" % (number % 8))
 
         lists = {}
         for name in ("offs", "n1", "n2", "k1", "n3", "n4"):
             lists[name] = held("list_" + name, [P, S // 16], U16)
 
-        x_table = held("x_table", [P, TABLE], I32)
-        x_byte_table = held("x_byte_table", [P, TABLE], U8)
+        x_table = held("x_table", [P, TABLE], I32, "x_table")
+        x_byte_table = held("x_byte_table", [P, TABLE], U8, "x_byte_table")
         d_table = held("d_table", [P, TABLE], I32)
         d_byte_table = held("d_byte_table", [P, TABLE], U8)
         w_raw = held("w_raw", [P, 2 * S], U8)
-        w_byte_raw = held("w_byte_raw", [P, S], U8)
+        w_byte_raw = held("w_byte_raw", [P, S], U8, "w_byte_raw")
         gain = held("gain", [P, PACK], F32)
         d_bytes = held("d_bytes", [P, S], U8)
 
@@ -68,44 +56,50 @@ def tile_picked_denseminmodover_none_po_kernel(
         nc.vector.memset(d_bytes[:].bitcast(I32), 0)
 
         nc.sync.dma_start(lists["offs"][:], offs)
+        nc.sync.dma_start(x_table[:], x_words[0].rearrange("p n t -> p (n t)").bitcast(I32))
+        nc.sync.dma_start(w_raw[:].bitcast(I32), w1_words[0].bitcast(I32))
+        nc.sync.dma_start(gain[:], gs.rearrange("(p t) o -> p (t o)", t=PACK))
         for q in range(4):
             nc.scalar.dma_start(
                 x_byte_table[32 * q : 32 * q + 4, :].bitcast(I32), x_scales[0, 4 * q : 4 * q + 4, :].bitcast(I32)
             )
-        nc.sync.dma_start(w_raw[:].bitcast(I32), w1_words[0].bitcast(I32))
-        nc.sync.dma_start(x_table[:], x_words[0].rearrange("p n t -> p (n t)").bitcast(I32))
         for q in range(4):
-            nc.scalar.dma_start(
+            nc.sync.dma_start(
                 w_byte_raw[32 * q : 32 * q + 4, :].bitcast(I32), w1_scales[0, 4 * q : 4 * q + 4, :].bitcast(I32)
             )
-        nc.sync.dma_start(gain[:], gs.rearrange("(p t) o -> p (t o)", t=PACK))
+        nc.sync.dma_start(d_byte_table[0:P:8, :].bitcast(I32), d_scales[0].bitcast(I32))
+        nc.sync.dma_start(lists["k1"][:], k1)
         nc.sync.dma_start(lists["n1"][:], n1)
         nc.sync.dma_start(lists["n2"][:], n2)
         nc.sync.dma_start(d_table[:], d_words[0].rearrange("p n t -> p (n t)").bitcast(I32))
-        nc.sync.dma_start(lists["k1"][:], k1)
-        nc.sync.dma_start(d_byte_table[0:P:8, :].bitcast(I32), d_scales[0].bitcast(I32))
         nc.sync.dma_start(lists["n3"][:], n3)
         nc.sync.dma_start(lists["n4"][:], n4)
 
-        x_bytes = held("x_bytes", [P, S], U8)
-        nc.vector.tensor_copy(x_bytes[:], x_byte_table[:].indirect(lists["offs"][:]))
+        y = [held("y%d" % t, [P, 2 * S if t < 2 else S], F32) for t in range(PACK)]
+        h = [held("h%d" % t, [P, 2 * S if t < LAST else S], F32) for t in range(PACK)]
+        for t in range(2):
+            nc.vector.memset(y[t][:, S:], 0.0)
+        for t in range(LAST):
+            nc.gpsimd.memset(h[t][:, S:], 0.0)
+
         w_codes = held("w_codes", [P, 2 * S], U8)
         nc.scalar.copy(
             w_codes[:].bitcast(U16).rearrange("p (t m) -> p t m", t=PACK),
             w_raw[:].bitcast(U16).rearrange("p (m t) -> p t m", t=PACK),
         )
-        w_bytes = held("w_bytes", [P, S], U8)
+        x_codes = held("x_codes", [P, S], U32)
+        nc.vector.tensor_copy(x_codes[:], x_table[:].bitcast(U32).indirect(lists["offs"][:]))
+        x_bytes = held("x_bytes", [P, S], U8, "x_table")
+        nc.vector.tensor_copy(x_bytes[:], x_byte_table[:].indirect(lists["offs"][:]))
+        w_bytes = held("w_bytes", [P, S], U8, "x_byte_table")
         nc.vector.tensor_copy(
             w_bytes[:].rearrange("p (t m) -> p t m", t=PACK), w_byte_raw[:].rearrange("p (m t) -> p t m", t=PACK)
         )
-        x_codes = held("x_codes", [P, S], U32)
-        nc.vector.tensor_copy(x_codes[:], x_table[:].bitcast(U32).indirect(lists["offs"][:]))
 
-        y = []
+        y_acc = [bank(t, "y_acc%d" % t, [P, S]) for t in range(PACK)]
         for t in range(PACK):
-            acc = bank(t, "y_acc%d" % t, S)
             nc.tensor.matmul_mx(
-                acc[:],
+                y_acc[t][:],
                 lhsT=w_codes[:, 2 * P * t : 2 * P * (t + 1)].bitcast(FP4X4),
                 lhsT_scale=w_bytes[:, P * t : P * (t + 1)],
                 rhs=x_codes[:].bitcast(FP8X4),
@@ -113,69 +107,102 @@ def tile_picked_denseminmodover_none_po_kernel(
                 start=True,
                 stop=True,
             )
-            row = held("y%d" % t, [P, S], F32)
-            if t == 1:
-                nc.vector.tensor_scalar(row[:], acc[:], gain[:, t : t + 1], None, ALU.mult)
+
+        def leave_y_bank(t):
+            if t in (1,):
+                nc.vector.tensor_scalar(y[t][:, :S], y_acc[t][:], gain[:, t : t + 1], None, ALU.mult)
             else:
-                nc.scalar.activation(row[:], acc[:], COPY, scale=gain[:, t : t + 1])
-            y.append(row)
+                nc.scalar.activation(y[t][:, :S], y_acc[t][:], COPY, scale=gain[:, t : t + 1])
 
-        d_picked_bytes = held("d_picked_bytes", [P, S], U8)
-        nc.vector.tensor_copy(d_picked_bytes[:], d_byte_table[:].indirect(lists["k1"][:]))
+        d_picked_bytes = held("d_picked_bytes", [P, S], U8, "w_byte_raw")
         d_picked = held("d_picked", [P, S], U32)
-        nc.vector.tensor_copy(d_picked[:], d_table[:].bitcast(U32).indirect(lists["k1"][:]))
         d_dealt_bytes = held("d_dealt_bytes", [P, S], U8)
-        nc.vector.tensor_copy(
-            d_dealt_bytes[:].rearrange("p (t m) -> p t m", t=PACK),
-            d_picked_bytes[:].rearrange("p (m t) -> p t m", t=PACK),
-        )
-        for r in range(4):
-            nc.sync.dma_start(d_bytes[r:P:32, :].bitcast(I32), d_dealt_bytes[8 * r : P : 32, :].bitcast(I32))
         d_codes = held("d_codes", [P, S], U32)
-        nc.vector.tensor_copy(
-            d_codes[:].rearrange("p (t m) -> p m t", t=PACK), d_picked[:].rearrange("p (m t) -> p m t", t=PACK)
-        )
 
-        h = [held("h%d" % t, [P, S], F32) for t in range(PACK)]
+        def pick_dictionary_bytes():
+            nc.vector.tensor_copy(d_picked_bytes[:], d_byte_table[:].indirect(lists["k1"][:]))
+
+        def deal_dictionary_bytes():
+            nc.vector.tensor_copy(
+                d_dealt_bytes[:].rearrange("p (t m) -> p t m", t=PACK),
+                d_picked_bytes[:].rearrange("p (m t) -> p t m", t=PACK),
+            )
+            for r in range(4):
+                nc.sync.dma_start(d_bytes[r:P:32, :].bitcast(I32), d_dealt_bytes[8 * r : P : 32, :].bitcast(I32))
+
+        def pick_dictionary_words():
+            nc.vector.tensor_copy(d_picked[:], d_table[:].bitcast(U32).indirect(lists["k1"][:]))
+
+        def deal_dictionary_words():
+            nc.vector.tensor_copy(
+                d_codes[:].rearrange("p (t c i) -> p c t i", t=PACK, i=4),
+                d_picked[:].rearrange("p (c i t) -> p c t i", t=PACK, i=4),
+            )
+
         z_codes = held("z_codes", [P, S], U32)
         z_bytes = held("z_bytes", [P, S], U8)
+        pa = held("pa", [P, PACK, S], BF16)
+        pb = held("pb", [P, PACK, S], BF16)
+        below = held("below", [P, PACK, S], BF16)
+        above = held("above", [P, PACK, S], BF16)
+        raised = held("raised", [P, PACK, S], BF16)
+        z_rows = held("z_rows", [P, PACK, S], BF16)
+        every, left, right = slice(0, S), slice(0, HALF), slice(HALF, S)
+        early, late = slice(0, 2), slice(2, 4)
 
-        steps = [(c, t) for c in range(len(FIRST_CHUNKS)) for t in range(PACK)]
-        pa, pb, low, z_rows = {}, {}, {}, {}
+        def fetch(engine, table, name, t, cols):
+            got = held("%s_%d_%d" % (name, t, cols.start), [P, cols.stop - cols.start], F32)
+            window = table[t][:].indirect(lists[name][:, cols.start // 16 : cols.stop // 16])
+            if engine is nc.vector:
+                nc.vector.tensor_copy(got[:], window)
+            else:
+                nc.scalar.activation(got[:], window, COPY)
+            return got
 
-        def fetch_first(c, t):
-            start, width = FIRST_CHUNKS[c]
-            a = held("a%d_%d" % (c, t), [P, width], F32)
-            b = held("b%d_%d" % (c, t), [P, width], F32)
-            nc.scalar.activation(a[:], y[t][:].indirect(entries(lists["n1"], start, width)), COPY)
-            nc.scalar.activation(b[:], y[t][:].indirect(entries(lists["n2"], start, width)), COPY)
-            return a, b
+        pick_dictionary_bytes()
+        near = {}
+        for t, cols in ((0, every), (1, every), (2, left), (3, left), (2, right), (3, right)):
+            if cols.start == 0:
+                leave_y_bank(t)
+            for name in ("n1", "n2"):
+                near[name, t, cols.start] = fetch(nc.scalar, y, name, t, cols)
 
-        def clamp_low(c, t):
-            width = FIRST_CHUNKS[c][1]
-            low[c, t] = held("low%d_%d" % (c, t), [P, width], F32)
-            nc.vector.scalar_tensor_tensor(low[c, t][:], pa[c, t][:], 0.0, pb[c, t][:], ALU.min, ALU.max)
+        def first_difference(t, cols):
+            nc.vector.tensor_tensor(pa[:, t, cols], y[t][:, cols], near["n1", t, cols.start][:], ALU.subtract)
 
-        def clamp_high(c, t):
-            start, width = FIRST_CHUNKS[c]
-            if t == 0:
-                z_rows[c] = held("z_rows%d" % c, [P, PACK, width], BF16)
-            nc.vector.scalar_tensor_tensor(z_rows[c][:, t, :], pa[c, t][:], 0.0, low[c, t][:], ALU.max, ALU.min)
-            if t == PACK - 1:
-                second_product(c)
+        def second_difference(t, cols):
+            nc.vector.tensor_tensor(pb[:, t, cols], near["n2", t, cols.start][:], y[t][:, cols], ALU.subtract)
 
-        def second_product(c):
-            start, width = FIRST_CHUNKS[c]
-            cols = slice(start, start + width)
-            grouped = held("z_grouped%d" % c, [P, width, PACK], BF16)
-            interleave(nc, grouped, z_rows[c])
-            nc.vector.quantize_mx(
-                z_codes[:, cols].bitcast(FP8X4), z_bytes[:, cols], grouped[:].rearrange("p j t -> p (j t)")
-            )
+        def bounds(rows, cols):
+            nc.vector.tensor_scalar(below[:, rows, cols], pa[:, rows, cols], 0.0, None, ALU.min)
+            nc.vector.tensor_scalar(above[:, rows, cols], pa[:, rows, cols], 0.0, None, ALU.max)
+
+        def clamp_low(rows, cols):
+            nc.vector.tensor_tensor(raised[:, rows, cols], below[:, rows, cols], pb[:, rows, cols], ALU.max)
+
+        def clamp_high(rows, cols):
+            nc.vector.tensor_tensor(z_rows[:, rows, cols], above[:, rows, cols], raised[:, rows, cols], ALU.min)
+
+        def weave(engine, name, rows, cols):
+            grouped = held("%s%d" % (name, cols.start), [P, HALF, PACK], BF16)
+            dst = grouped[:].rearrange("p (c i) t -> p c t i", i=4)
+            src = rows[:, :, cols].rearrange("p t (c i) -> p c t i", i=4)
+            if engine is nc.vector:
+                nc.vector.tensor_copy(dst, src)
+            else:
+                nc.scalar.copy(dst, src)
+            return grouped[:].rearrange("p j t -> p (j t)")
+
+        h_acc = {}
+
+        def second_product(grouped, cols):
+            nc.vector.quantize_mx(z_codes[:, cols].bitcast(FP8X4), z_bytes[:, cols], grouped)
             for t in range(PACK):
-                acc = bank(4 + 4 * c + t, "h_acc%d_%d" % (c, t), width)
+                h_acc[t, cols.start] = bank(
+                    t + (4 if cols.start == 0 else 0), "h_acc%d_%d" % (t, cols.start), [P, HALF]
+                )
                 nc.tensor.matmul_mx(
-                    acc[:],
+                    h_acc[t, cols.start][:],
                     lhsT=d_codes[:, P * t : P * (t + 1)].bitcast(FP8X4),
                     lhsT_scale=d_bytes[:, P * t : P * (t + 1)],
                     rhs=z_codes[:, cols].bitcast(FP8X4),
@@ -183,64 +210,95 @@ def tile_picked_denseminmodover_none_po_kernel(
                     start=True,
                     stop=True,
                 )
-                if c == len(FIRST_CHUNKS) - 1 and t % 2 == 1:
-                    nc.vector.tensor_scalar(h[t][:, cols], acc[:], 0.0625, None, ALU.mult)
-                else:
-                    nc.scalar.activation(h[t][:, cols], acc[:], COPY, scale=0.0625)
 
-        for s in range(len(steps) + 2):
-            if s < len(steps):
-                c, t = steps[s]
-                start, width = FIRST_CHUNKS[c]
-                cols = slice(start, start + width)
-                a, b = fetch_first(c, t)
-                pa[c, t] = held("pa%d_%d" % (c, t), [P, width], F32)
-                pb[c, t] = held("pb%d_%d" % (c, t), [P, width], F32)
-                nc.vector.tensor_tensor(pa[c, t][:], y[t][:, cols], a[:], ALU.subtract)
-            if s >= 2:
-                clamp_high(*steps[s - 2])
-            if s < len(steps):
-                nc.vector.tensor_tensor(pb[c, t][:], b[:], y[t][:, cols], ALU.subtract)
-            if 1 <= s <= len(steps):
-                clamp_low(*steps[s - 1])
+        def leave_h_bank(engine, t, cols):
+            if engine is nc.vector:
+                nc.vector.tensor_scalar(h[t][:, cols], h_acc[t, cols.start][:], 0.0625, None, ALU.mult)
+            else:
+                nc.scalar.activation(h[t][:, cols], h_acc[t, cols.start][:], COPY, scale=0.0625)
+
+        first_difference(0, every)
+        deal_dictionary_bytes()
+        second_difference(0, every)
+        pick_dictionary_words()
+        first_difference(1, every)
+        deal_dictionary_words()
+        second_difference(1, every)
+        bounds(early, every)
+        first_difference(2, left)
+        clamp_low(early, every)
+        second_difference(2, left)
+        clamp_high(early, every)
+        first_difference(3, left)
+        second_difference(3, left)
+        bounds(late, left)
+        first_difference(2, right)
+        clamp_low(late, left)
+        second_difference(2, right)
+        clamp_high(late, left)
+        z_left = weave(nc.scalar, "z_grouped", z_rows, left)
+        first_difference(3, right)
+        second_difference(3, right)
+        bounds(late, right)
+        clamp_low(late, right)
+        clamp_high(late, right)
+        second_product(z_left, left)
+        second_product(weave(nc.vector, "z_grouped", z_rows, right), right)
+        for t in range(PACK):
+            leave_h_bank(nc.scalar, t, left)
 
         out_codes = held("out_codes", [P, S], U32)
         out_bytes = held("out_bytes", [P, S], U8)
         out_rows = out_0.rearrange("(p t) j -> p t j", t=PACK)
         out_words = out_1[0].rearrange("p n t -> p (n t)").bitcast(I32)
-        steps = [(c, t) for c in range(len(SECOND_CHUNKS)) for t in range(PACK)]
-        larger, result = {}, {}
+        result = held("result", [P, PACK, S], F32)
+        far, larger = {}, {}
 
-        def finish(c, t):
-            start, width = SECOND_CHUNKS[c]
-            cols = slice(start, start + width)
-            if t == 0:
-                result[c] = held("result%d" % c, [P, PACK, width], F32)
-            nc.vector.scalar_tensor_tensor(result[c][:, t, :], h[t][:, cols], -0.75, larger[c, t][:], ALU.mult, ALU.add)
-            if t == PACK - 1:
-                nc.sync.dma_start(out_rows[:, :, cols], result[c][:])
-                grouped = held("out_grouped%d" % c, [P, width, PACK], BF16)
-                interleave(nc, grouped, result[c])
-                nc.vector.quantize_mx(
-                    out_codes[:, cols].bitcast(FP8X4), out_bytes[:, cols], grouped[:].rearrange("p j t -> p (j t)")
-                )
-                nc.sync.dma_start(out_words[:, cols], out_codes[:, cols].bitcast(I32))
+        leave_h_bank(nc.scalar, 0, right)
+        leave_h_bank(nc.vector, 1, right)
+        far["n4", 1, 0] = fetch(nc.vector, h, "n4", 1, every)
+        far["n4", 0, 0] = fetch(nc.vector, h, "n4", 0, every)
+        far["n3", 0, 0] = fetch(nc.scalar, h, "n3", 0, every)
+        far["n3", 1, 0] = fetch(nc.scalar, h, "n3", 1, every)
+        leave_h_bank(nc.scalar, 2, right)
+        leave_h_bank(nc.scalar, 3, right)
+        far["n3", 2, 0] = fetch(nc.scalar, h, "n3", 2, every)
+        far["n4", 2, 0] = fetch(nc.scalar, h, "n4", 2, every)
+        far["n3", 3, 0] = fetch(nc.scalar, h, "n3", 3, left)
+        far["n3", 3, HALF] = fetch(nc.scalar, h, "n3", 3, right)
+        far["n4", 3, HALF] = fetch(nc.scalar, h, "n4", 3, right)
 
-        for s in range(len(steps) + 1):
-            if s < len(steps):
-                c, t = steps[s]
-                start, width = SECOND_CHUNKS[c]
-                third = held("third%d_%d" % (c, t), [P, width], F32)
-                fourth = held("fourth%d_%d" % (c, t), [P, width], F32)
-                nc.scalar.activation(third[:], h[t][:].indirect(entries(lists["n3"], start, width)), COPY)
-                if s < VECTOR_FETCHES:
-                    nc.vector.tensor_copy(fourth[:], h[t][:].indirect(entries(lists["n4"], start, width)))
-                else:
-                    nc.scalar.activation(fourth[:], h[t][:].indirect(entries(lists["n4"], start, width)), COPY)
-                larger[c, t] = held("larger%d_%d" % (c, t), [P, width], F32)
-                nc.vector.tensor_tensor(larger[c, t][:], third[:], fourth[:], ALU.max)
-            if s >= 1:
-                finish(*steps[s - 1])
+        def take_larger(t, cols):
+            larger[t, cols.start] = held("larger%d_%d" % (t, cols.start), [P, cols.stop - cols.start], F32)
+            nc.vector.tensor_tensor(
+                larger[t, cols.start][:], far["n3", t, cols.start][:], far["n4", t, cols.start][:], ALU.max
+            )
+
+        def finish(t, cols):
+            nc.vector.scalar_tensor_tensor(
+                result[:, t, cols], h[t][:, cols], -0.75, larger[t, cols.start][:], ALU.mult, ALU.add
+            )
+            nc.sync.dma_start(out_rows[:, t, cols], result[:, t, cols])
+
+        def hand_on(grouped, cols):
+            nc.vector.quantize_mx(out_codes[:, cols].bitcast(FP8X4), out_bytes[:, cols], grouped)
+            nc.sync.dma_start(out_words[:, cols], out_codes[:, cols].bitcast(I32))
+
+        take_larger(0, every)
+        take_larger(1, every)
+        finish(0, every)
+        finish(1, every)
+        far["n4", 3, 0] = fetch(nc.vector, h, "n4", 3, left)
+        take_larger(2, every)
+        take_larger(3, left)
+        finish(2, every)
+        finish(3, left)
+        out_left = weave(nc.scalar, "out_grouped", result, left)
+        take_larger(3, right)
+        finish(3, right)
+        out_right = weave(nc.vector, "out_grouped", result, right)
+        hand_on(out_left, left)
+        hand_on(out_right, right)
 
         for q in range(4):
             queue = nc.sync if q % 2 == 0 else nc.scalar

from contextlib import ExitStack

import concourse.mybir as mybir

F32 = mybir.dt.float32
BF16 = mybir.dt.bfloat16
I32 = mybir.dt.int32
U32 = mybir.dt.uint32
U16 = mybir.dt.uint16
U8 = mybir.dt.uint8
FP8X4 = mybir.dt.float8_e4m3fn_x4
FP4X4 = mybir.dt.float4_e2m1fn_x4
ALU = mybir.AluOpType
COPY = mybir.ActivationFunctionType.Copy

P = 128
PACK = 4
S = 512
TABLE = 2048
FLOPS = 2 * 2 * 512 * 512 * 512

LAST = PACK - 1
HALF = S // 2


def tile_picked_denseminmodover_none_po_kernel(
    tc, x_words, x_scales, w1_words, w1_scales, gs, d_words, d_scales, offs, n1, n2, k1, n3, n4, out_0, out_1, out_2
):
    nc = tc.nc
    with ExitStack() as ctx:
        keep = ctx.enter_context(tc.tile_pool(name="keep", bufs=1))
        psum = ctx.enter_context(tc.psum_pool(name="psum", bufs=1))

        def held(name, shape, dtype, tag=None):
            return keep.tile(shape, dtype, name=name, tag=tag or name, align_bytes=64)

        def bank(number, name, shape):
            return psum.tile(shape, F32, name=name, tag="bank%d" % (number % 8))

        lists = {}
        for name in ("offs", "n1", "n2", "k1", "n3", "n4"):
            lists[name] = held("list_" + name, [P, S // 16], U16)

        x_table = held("x_table", [P, TABLE], I32, "x_table")
        x_byte_table = held("x_byte_table", [P, TABLE], U8, "x_byte_table")
        d_table = held("d_table", [P, TABLE], I32)
        d_byte_table = held("d_byte_table", [P, TABLE], U8)
        w_raw = held("w_raw", [P, 2 * S], U8)
        w_byte_raw = held("w_byte_raw", [P, S], U8, "w_byte_raw")
        gain = held("gain", [P, PACK], F32)
        d_bytes = held("d_bytes", [P, S], U8)

        nc.gpsimd.memset(x_byte_table[:].bitcast(I32), 0)
        nc.gpsimd.memset(w_byte_raw[:].bitcast(I32), 0)
        nc.vector.memset(d_byte_table[:].bitcast(I32), 0)
        nc.vector.memset(d_bytes[:].bitcast(I32), 0)

        nc.sync.dma_start(lists["offs"][:], offs)
        nc.sync.dma_start(x_table[:], x_words[0].rearrange("p n t -> p (n t)").bitcast(I32))
        nc.sync.dma_start(w_raw[:].bitcast(I32), w1_words[0].bitcast(I32))
        nc.sync.dma_start(gain[:], gs.rearrange("(p t) o -> p (t o)", t=PACK))
        for q in range(4):
            nc.scalar.dma_start(
                x_byte_table[32 * q : 32 * q + 4, :].bitcast(I32), x_scales[0, 4 * q : 4 * q + 4, :].bitcast(I32)
            )
        for q in range(4):
            nc.sync.dma_start(
                w_byte_raw[32 * q : 32 * q + 4, :].bitcast(I32), w1_scales[0, 4 * q : 4 * q + 4, :].bitcast(I32)
            )
        nc.sync.dma_start(d_byte_table[0:P:8, :].bitcast(I32), d_scales[0].bitcast(I32))
        nc.sync.dma_start(lists["k1"][:], k1)
        nc.sync.dma_start(lists["n1"][:], n1)
        nc.sync.dma_start(lists["n2"][:], n2)
        nc.sync.dma_start(d_table[:], d_words[0].rearrange("p n t -> p (n t)").bitcast(I32))
        nc.sync.dma_start(lists["n3"][:], n3)
        nc.sync.dma_start(lists["n4"][:], n4)

        y = [held("y%d" % t, [P, 2 * S if t < 2 else S], F32) for t in range(PACK)]
        h = [held("h%d" % t, [P, 2 * S if t < LAST else S], F32) for t in range(PACK)]
        for t in range(2):
            nc.vector.memset(y[t][:, S:], 0.0)
        for t in range(LAST):
            nc.gpsimd.memset(h[t][:, S:], 0.0)

        w_codes = held("w_codes", [P, 2 * S], U8)
        nc.scalar.copy(
            w_codes[:].bitcast(U16).rearrange("p (t m) -> p t m", t=PACK),
            w_raw[:].bitcast(U16).rearrange("p (m t) -> p t m", t=PACK),
        )
        x_codes = held("x_codes", [P, S], U32)
        nc.vector.tensor_copy(x_codes[:], x_table[:].bitcast(U32).indirect(lists["offs"][:]))
        x_bytes = held("x_bytes", [P, S], U8, "x_table")
        nc.vector.tensor_copy(x_bytes[:], x_byte_table[:].indirect(lists["offs"][:]))
        w_bytes = held("w_bytes", [P, S], U8, "x_byte_table")
        nc.vector.tensor_copy(
            w_bytes[:].rearrange("p (t m) -> p t m", t=PACK), w_byte_raw[:].rearrange("p (m t) -> p t m", t=PACK)
        )

        y_acc = [bank(t, "y_acc%d" % t, [P, S]) for t in range(PACK)]
        for t in range(PACK):
            nc.tensor.matmul_mx(
                y_acc[t][:],
                lhsT=w_codes[:, 2 * P * t : 2 * P * (t + 1)].bitcast(FP4X4),
                lhsT_scale=w_bytes[:, P * t : P * (t + 1)],
                rhs=x_codes[:].bitcast(FP8X4),
                rhs_scale=x_bytes[:],
                start=True,
                stop=True,
            )

        def leave_y_bank(t):
            if t in (1,):
                nc.vector.tensor_scalar(y[t][:, :S], y_acc[t][:], gain[:, t : t + 1], None, ALU.mult)
            else:
                nc.scalar.activation(y[t][:, :S], y_acc[t][:], COPY, scale=gain[:, t : t + 1])

        d_picked_bytes = held("d_picked_bytes", [P, S], U8, "w_byte_raw")
        d_picked = held("d_picked", [P, S], U32)
        d_dealt_bytes = held("d_dealt_bytes", [P, S], U8)
        d_codes = held("d_codes", [P, S], U32)

        def pick_dictionary_bytes():
            nc.vector.tensor_copy(d_picked_bytes[:], d_byte_table[:].indirect(lists["k1"][:]))

        def deal_dictionary_bytes():
            nc.vector.tensor_copy(
                d_dealt_bytes[:].rearrange("p (t m) -> p t m", t=PACK),
                d_picked_bytes[:].rearrange("p (m t) -> p t m", t=PACK),
            )
            for r in range(4):
                nc.sync.dma_start(d_bytes[r:P:32, :].bitcast(I32), d_dealt_bytes[8 * r : P : 32, :].bitcast(I32))

        def pick_dictionary_words():
            nc.vector.tensor_copy(d_picked[:], d_table[:].bitcast(U32).indirect(lists["k1"][:]))

        def deal_dictionary_words():
            nc.vector.tensor_copy(
                d_codes[:].rearrange("p (t c i) -> p c t i", t=PACK, i=4),
                d_picked[:].rearrange("p (c i t) -> p c t i", t=PACK, i=4),
            )

        z_codes = held("z_codes", [P, S], U32)
        z_bytes = held("z_bytes", [P, S], U8)
        pa = held("pa", [P, PACK, S], BF16)
        pb = held("pb", [P, PACK, S], BF16)
        below = held("below", [P, PACK, S], BF16)
        above = held("above", [P, PACK, S], BF16)
        raised = held("raised", [P, PACK, S], BF16)
        z_rows = held("z_rows", [P, PACK, S], BF16)
        every, left, right = slice(0, S), slice(0, HALF), slice(HALF, S)
        early, late = slice(0, 2), slice(2, 4)

        def fetch(engine, table, name, t, cols):
            got = held("%s_%d_%d" % (name, t, cols.start), [P, cols.stop - cols.start], F32)
            window = table[t][:].indirect(lists[name][:, cols.start // 16 : cols.stop // 16])
            if engine is nc.vector:
                nc.vector.tensor_copy(got[:], window)
            else:
                nc.scalar.activation(got[:], window, COPY)
            return got

        pick_dictionary_bytes()
        near = {}
        for t, cols in ((0, every), (1, every), (2, left), (3, left), (2, right), (3, right)):
            if cols.start == 0:
                leave_y_bank(t)
            for name in ("n1", "n2"):
                near[name, t, cols.start] = fetch(nc.scalar, y, name, t, cols)

        def first_difference(t, cols):
            nc.vector.tensor_tensor(pa[:, t, cols], y[t][:, cols], near["n1", t, cols.start][:], ALU.subtract)

        def second_difference(t, cols):
            nc.vector.tensor_tensor(pb[:, t, cols], near["n2", t, cols.start][:], y[t][:, cols], ALU.subtract)

        def bounds(rows, cols):
            nc.vector.tensor_scalar(below[:, rows, cols], pa[:, rows, cols], 0.0, None, ALU.min)
            nc.vector.tensor_scalar(above[:, rows, cols], pa[:, rows, cols], 0.0, None, ALU.max)

        def clamp_low(rows, cols):
            nc.vector.tensor_tensor(raised[:, rows, cols], below[:, rows, cols], pb[:, rows, cols], ALU.max)

        def clamp_high(rows, cols):
            nc.vector.tensor_tensor(z_rows[:, rows, cols], above[:, rows, cols], raised[:, rows, cols], ALU.min)

        def weave(engine, name, rows, cols):
            grouped = held("%s%d" % (name, cols.start), [P, HALF, PACK], BF16)
            dst = grouped[:].rearrange("p (c i) t -> p c t i", i=4)
            src = rows[:, :, cols].rearrange("p t (c i) -> p c t i", i=4)
            if engine is nc.vector:
                nc.vector.tensor_copy(dst, src)
            else:
                nc.scalar.copy(dst, src)
            return grouped[:].rearrange("p j t -> p (j t)")

        h_acc = {}

        def second_product(grouped, cols):
            nc.vector.quantize_mx(z_codes[:, cols].bitcast(FP8X4), z_bytes[:, cols], grouped)
            for t in range(PACK):
                h_acc[t, cols.start] = bank(
                    t + (4 if cols.start == 0 else 0), "h_acc%d_%d" % (t, cols.start), [P, HALF]
                )
                nc.tensor.matmul_mx(
                    h_acc[t, cols.start][:],
                    lhsT=d_codes[:, P * t : P * (t + 1)].bitcast(FP8X4),
                    lhsT_scale=d_bytes[:, P * t : P * (t + 1)],
                    rhs=z_codes[:, cols].bitcast(FP8X4),
                    rhs_scale=z_bytes[:, cols],
                    start=True,
                    stop=True,
                )

        def leave_h_bank(engine, t, cols):
            if engine is nc.vector:
                nc.vector.tensor_scalar(h[t][:, cols], h_acc[t, cols.start][:], 0.0625, None, ALU.mult)
            else:
                nc.scalar.activation(h[t][:, cols], h_acc[t, cols.start][:], COPY, scale=0.0625)

        first_difference(0, every)
        deal_dictionary_bytes()
        second_difference(0, every)
        pick_dictionary_words()
        first_difference(1, every)
        deal_dictionary_words()
        second_difference(1, every)
        bounds(early, every)
        first_difference(2, left)
        clamp_low(early, every)
        second_difference(2, left)
        clamp_high(early, every)
        first_difference(3, left)
        second_difference(3, left)
        bounds(late, left)
        first_difference(2, right)
        clamp_low(late, left)
        second_difference(2, right)
        clamp_high(late, left)
        z_left = weave(nc.scalar, "z_grouped", z_rows, left)
        first_difference(3, right)
        second_difference(3, right)
        bounds(late, right)
        clamp_low(late, right)
        clamp_high(late, right)
        second_product(z_left, left)
        second_product(weave(nc.vector, "z_grouped", z_rows, right), right)
        for t in range(PACK):
            leave_h_bank(nc.scalar, t, left)

        out_codes = held("out_codes", [P, S], U32)
        out_bytes = held("out_bytes", [P, S], U8)
        out_rows = out_0.rearrange("(p t) j -> p t j", t=PACK)
        out_words = out_1[0].rearrange("p n t -> p (n t)").bitcast(I32)
        result = held("result", [P, PACK, S], F32)
        far, larger = {}, {}

        leave_h_bank(nc.scalar, 0, right)
        leave_h_bank(nc.vector, 1, right)
        far["n4", 1, 0] = fetch(nc.vector, h, "n4", 1, every)
        far["n4", 0, 0] = fetch(nc.vector, h, "n4", 0, every)
        far["n3", 0, 0] = fetch(nc.scalar, h, "n3", 0, every)
        far["n3", 1, 0] = fetch(nc.scalar, h, "n3", 1, every)
        leave_h_bank(nc.scalar, 2, right)
        leave_h_bank(nc.scalar, 3, right)
        far["n3", 2, 0] = fetch(nc.scalar, h, "n3", 2, every)
        far["n4", 2, 0] = fetch(nc.scalar, h, "n4", 2, every)
        far["n3", 3, 0] = fetch(nc.scalar, h, "n3", 3, left)
        far["n3", 3, HALF] = fetch(nc.scalar, h, "n3", 3, right)
        far["n4", 3, HALF] = fetch(nc.scalar, h, "n4", 3, right)

        def take_larger(t, cols):
            larger[t, cols.start] = held("larger%d_%d" % (t, cols.start), [P, cols.stop - cols.start], F32)
            nc.vector.tensor_tensor(
                larger[t, cols.start][:], far["n3", t, cols.start][:], far["n4", t, cols.start][:], ALU.max
            )

        def finish(t, cols):
            nc.vector.scalar_tensor_tensor(
                result[:, t, cols], h[t][:, cols], -0.75, larger[t, cols.start][:], ALU.mult, ALU.add
            )
            nc.sync.dma_start(out_rows[:, t, cols], result[:, t, cols])

        def hand_on(grouped, cols):
            nc.vector.quantize_mx(out_codes[:, cols].bitcast(FP8X4), out_bytes[:, cols], grouped)
            nc.sync.dma_start(out_words[:, cols], out_codes[:, cols].bitcast(I32))

        take_larger(0, every)
        take_larger(1, every)
        finish(0, every)
        finish(1, every)
        far["n4", 3, 0] = fetch(nc.vector, h, "n4", 3, left)
        take_larger(2, every)
        take_larger(3, left)
        finish(2, every)
        finish(3, left)
        out_left = weave(nc.scalar, "out_grouped", result, left)
        take_larger(3, right)
        finish(3, right)
        out_right = weave(nc.vector, "out_grouped", result, right)
        hand_on(out_left, left)
        hand_on(out_right, right)

        for q in range(4):
            queue = nc.sync if q % 2 == 0 else nc.scalar
            queue.dma_start(
                out_2[0, 4 * q : 4 * q + 4, :].bitcast(I32), out_bytes[32 * q : 32 * q + 4, :].bitcast(I32)
            )
